import numpy as np, ml_dtypes
CORES = [78,86,94,102,110,118]
N = 6
import mx_ref
NC, KT = 512, 3
OWNER = [0,5,0,5,5,5]
BF = ml_dtypes.bfloat16
def setup_inputs(rng):
    def f(*shape):
        return mx_ref.flush((rng.standard_normal(shape, dtype=np.float32) * np.exp2(rng.integers(-2, 3, shape[:-1] + (1,)))).astype(BF))
    return {"w": f(N, 128, KT * 512), "x": f(N, 128, KT * 4 * NC)}
def setup_inputs_blocks(rng):
    d = setup_inputs(rng)
    for k in ("w", "x"): d[k] = mx_ref.spread(d[k], rng, 1)
    return d
def setup_inputs_wide(rng):
    d = setup_inputs(rng)
    for k in ("w", "x"): d[k] = mx_ref.flush((d[k].astype(np.float32) * np.exp2(rng.integers(-8, 9, (N, 1, 1))).astype(np.float32)).astype(BF))
    return d
def setup_inputs_zeros(rng):
    d = setup_inputs(rng); v = d["x"].reshape(N, 128, -1, 4).copy()
    v[np.broadcast_to((rng.random((N, 1, v.shape[2], 1)) < 0.33), v.shape)] = 0
    d["x"] = v.reshape(d["x"].shape)
    return d
def reference(w, x):
    y = np.zeros((N, 128, NC), np.float32)
    for r in range(N):
        for t in range(KT):
            p = mx_ref.matmul(mx_ref.quantize(w[OWNER[r]][:, 512 * t:512 * t + 512]), mx_ref.quantize(x[r][:, 4 * NC * t:4 * NC * t + 4 * NC]))
            y[r] = p if t == 0 else y[r] + p
    return {"y": y}

@@ -1,0 +1,127 @@
+from concourse.bass import DstId, RemoteDMATransfer
+from concourse.mybir import dt, ActivationFunctionType
+
+KT = 3
+WC = 128
+NC = 512
+BLOCKS = [(0, 256), (256, 256)]
+ENGINES = 8
+
+SCRATCH = {
+    "wb": ("sbuf", [128, KT * 4 * WC], "bfloat16"),
+    "xb": ("sbuf", [128, KT * 4 * NC], "bfloat16"),
+    "wq": ("sbuf", [128, KT * WC], "float8_e4m3fn_x4"),
+    "ws": ("sbuf", [128, KT * WC], "uint8"),
+    "xq": ("sbuf", [128, KT * NC], "float8_e4m3fn_x4"),
+    "xs": ("sbuf", [128, KT * NC], "uint8"),
+    "ps": ("psum", [128, 512 * len(BLOCKS)], "float32"),
+    "yb": ("sbuf", [128, NC], "float32"),
+}
+SEMAPHORES = (["wl", "wqd", "warr", "sent"] + ["xl%d" % t for t in range(KT)] + ["xq%d" % t for t in range(KT)]
+              + ["mm%d" % b for b in range(len(BLOCKS))] + ["cp%d" % b for b in range(len(BLOCKS))]
+              + ["st%d" % b for b in range(len(BLOCKS))])
+
+
+def _pick(mask, n):
+    out, b, k = 0, 0, 0
+    while k < n:
+        if (mask >> b) & 1:
+            out |= 1 << b
+            k += 1
+        b += 1
+    return out
+
+
+def _count(mask):
+    return bin(mask).count("1")
+
+
+def _plan(T, topo):
+    cores, owner = list(T.cores), T.tables["OWNER"]
+    plan = {}
+    for o in sorted(set(owner)):
+        dsts = [cores[r] for r in range(len(cores)) if owner[r] == o and r != o]
+        if dsts:
+            plan[cores[o]] = [dsts]
+    return plan
+
+
+def _mask(topo, src, dsts):
+    m = topo.mask(src, dsts[0])
+    for d in dsts[1:]:
+        m &= topo.mask(src, d)
+    return _pick(m, ENGINES)
+
+
+def rank_program(g, core, T, topo):
+    plan = _plan(T, topo)
+    rank = T.rank_of(core)
+    if rank is None and core not in plan:
+        return
+    S = T.sem
+    is_owner = rank is not None and T.tables["OWNER"][rank] == rank
+    expect = 0
+    for src, calls in plan.items():
+        for dsts in calls:
+            if core in dsts:
+                expect += 2 * _count(_mask(topo, src, dsts))
+
+    if is_owner:
+        g.sync.dma_start(T.wb[:], T.w[:]).then_inc(S.wl, 16)
+    for t in range(KT):
+        q = g.sync if (is_owner or t % 2 == 0) else g.scalar
+        q.dma_start(T.xb[:, 4 * NC * t:4 * NC * (t + 1)], T.x[:, 4 * NC * t:4 * NC * (t + 1)]).then_inc(S["xl%d" % t], 16)
+
+    if is_owner:
+        g.vector.wait_ge(S.wl, 16)
+        g.vector.quantize_mx(T.wq[:], T.ws[:], T.wb[:]).then_inc(S.wqd, 1)
+    for t in range(KT):
+        g.vector.wait_ge(S["xl%d" % t], 16)
+        g.vector.quantize_mx(T.xq[:, NC * t:NC * (t + 1)], T.xs[:, NC * t:NC * (t + 1)],
+                             T.xb[:, 4 * NC * t:4 * NC * (t + 1)]).then_inc(S["xq%d" % t], 1)
+
+    if core in plan:
+        if is_owner:
+            g.wait_ge(S.wqd, 1)
+        else:
+            g.wait_ge(S.warr, expect)
+        left = 0
+        for dsts in plan[core]:
+            for d in dsts:
+                assert topo.may_write(core, d)
+            m = _mask(topo, core, dsts)
+            ids = [DstId(rid=topo.addr(d)[0], pnc=topo.addr(d)[1]) for d in dsts]
+            for ap in (T.wq[:].bitcast(dt.uint8), T.ws[:]):
+                g.remote_dma_fused([RemoteDMATransfer(dst_ids=ids, dma_engine_mask=m, remote_sem=S.warr,
+                                                      srcs=[ap], dsts=[ap for _ in dsts])], local_sem=S.sent)
+                left += _count(m)
+        g.wait_ge(S.sent, left)
+
+    if is_owner:
+        g.tensor.wait_ge(S.wqd, 1)
+    else:
+        g.tensor.wait_ge(S.warr, expect)
+    for b, (c0, n) in enumerate(BLOCKS):
+        for t in range(KT):
+            if b == 0:
+                g.tensor.wait_ge(S["xq%d" % t], 1)
+            mm = g.tensor.matmul_mx(T.ps[:, 512 * b:512 * b + n],
+                                    T.wq[:, WC * t:WC * (t + 1)], T.ws[:, WC * t:WC * (t + 1)],
+                                    T.xq[:, NC * t + c0:NC * t + c0 + n], T.xs[:, NC * t + c0:NC * t + c0 + n],
+                                    t == 0, t == KT - 1)
+        mm.then_inc(S["mm%d" % b], 1)
+    for b, (c0, n) in enumerate(BLOCKS):
+        mm, cp, st = S["mm%d" % b], S["cp%d" % b], S["st%d" % b]
+        if b % 2 == 0:
+            g.vector.wait_ge(mm, 1)
+            g.vector.tensor_copy(T.yb[:, c0:c0 + n], T.ps[:, 512 * b:512 * b + n]).then_inc(cp, 1)
+            q = g.sync
+        else:
+            g.scalar.wait_ge(mm, 1)
+            g.scalar.activation(T.yb[:, c0:c0 + n], T.ps[:, 512 * b:512 * b + n],
+                                ActivationFunctionType.Copy).then_inc(cp, 1)
+            q = g.scalar
+        q.wait_ge(cp, 1)
+        q.dma_start(T.y[:, c0:c0 + n], T.yb[:, c0:c0 + n]).then_inc(st, 16)
+    for b in range(len(BLOCKS)):
+        (g.sync if b % 2 == 0 else g.scalar).wait_ge(S["st%d" % b], 16)

@@ -5,7 +5,9 @@ KT = 3
 WC = 128
 NC = 512
 BLOCKS = [(0, 256), (256, 256)]
-ENGINES = 8
+PW = KT * WC // 4
+SAME_DIE = [True, False]
+OWN_WORDS = KT * WC - PW * (len(SAME_DIE) - 1)
 
 SCRATCH = {
     "wb": ("sbuf", [128, KT * 4 * WC], "bfloat16"),
@@ -17,18 +19,19 @@ SCRATCH = {
     "ps": ("psum", [128, 512 * len(BLOCKS)], "float32"),
     "yb": ("sbuf", [128, NC], "float32"),
 }
-SEMAPHORES = (["wl", "wqd", "warr", "sent"] + ["xl%d" % t for t in range(KT)] + ["xq%d" % t for t in range(KT)]
+SEMAPHORES = (["wl", "wqd", "warr", "hand", "sent"] + ["xl%d" % t for t in range(KT)] + ["xq%d" % t for t in range(KT)]
               + ["mm%d" % b for b in range(len(BLOCKS))] + ["cp%d" % b for b in range(len(BLOCKS))]
               + ["st%d" % b for b in range(len(BLOCKS))])
 
 
-def _pick(mask, n):
-    out, b, k = 0, 0, 0
-    while k < n:
-        if (mask >> b) & 1:
-            out |= 1 << b
-            k += 1
-        b += 1
+def _engines(mask):
+    return [b for b in range(mask.bit_length()) if (mask >> b) & 1]
+
+
+def _bits(engines):
+    out = 0
+    for b in engines:
+        out |= 1 << b
     return out
 
 
@@ -36,42 +39,71 @@ def _count(mask):
     return bin(mask).count("1")
 
 
+def _piece(T, p):
+    kind, a, b = p
+    return T.ws[:, a:b] if kind == "s" else T.wq[:, a:b].bitcast(dt.uint8)
+
+
 def _plan(T, topo):
     cores, owner = list(T.cores), T.tables["OWNER"]
     plan = {}
     for o in sorted(set(owner)):
+        src = cores[o]
         dsts = [cores[r] for r in range(len(cores)) if owner[r] == o and r != o]
-        if dsts:
-            plan[cores[o]] = [dsts]
+        if not dsts:
+            continue
+        off = topo.mask(src, dsts[0])
+        for d in dsts:
+            off &= topo.mask(src, d)
+        if len(dsts) < 3:
+            plan[src] = (dsts, off, [("q", 0, KT * WC), ("s", 0, KT * WC)], [])
+            continue
+        pieces = [("s", 0, KT * WC)] + [("q", a, a + PW) for a in range(OWN_WORDS, KT * WC, PW)]
+        helpers, used = [], []
+        for same in SAME_DIE:
+            h = [c for c in range(128) if topo.chip(c) == topo.chip(src) and c not in cores and c not in used
+                 and (topo.die(c) == topo.die(src)) == same and all(topo.may_write(c, d) for d in dsts)][0]
+            used.append(h)
+        free = _engines(topo.mask(src, used[0]) & ~off)
+        n = len(free) // len(used)
+        for i, h in enumerate(used):
+            helpers.append((h, _bits(free[n * i:n * (i + 1)]), pieces[i]))
+        plan[src] = (dsts, off, [("q", 0, OWN_WORDS)], helpers)
     return plan
-
-
-def _mask(topo, src, dsts):
-    m = topo.mask(src, dsts[0])
-    for d in dsts[1:]:
-        m &= topo.mask(src, d)
-    return _pick(m, ENGINES)
 
 
 def rank_program(g, core, T, topo):
     plan = _plan(T, topo)
     rank = T.rank_of(core)
-    if rank is None and core not in plan:
-        return
     S = T.sem
-    is_owner = rank is not None and T.tables["OWNER"][rank] == rank
+
+    def send(dsts, m, p, sem):
+        for d in dsts:
+            assert topo.may_write(core, d)
+        ids = [DstId(rid=topo.addr(d)[0], pnc=topo.addr(d)[1]) for d in dsts]
+        return RemoteDMATransfer(dst_ids=ids, dma_engine_mask=m, remote_sem=sem,
+                                 srcs=[_piece(T, p)], dsts=[_piece(T, p) for _ in dsts])
+
+    if rank is None:
+        for src, (dsts, off, own, helpers) in plan.items():
+            for h, m, p in helpers:
+                if h == core:
+                    g.wait_ge(S.hand, _count(m))
+                    g.remote_dma_fused([send(dsts, off, p, S.warr)], local_sem=S.sent)
+                    g.wait_ge(S.sent, _count(off))
+        return
+
+    is_owner = T.tables["OWNER"][rank] == rank
     expect = 0
-    for src, calls in plan.items():
-        for dsts in calls:
-            if core in dsts:
-                expect += 2 * _count(_mask(topo, src, dsts))
+    for src, (dsts, off, own, helpers) in plan.items():
+        if core in dsts:
+            expect = _count(off) * (len(own) + len(helpers))
 
     if is_owner:
         g.sync.dma_start(T.wb[:], T.w[:]).then_inc(S.wl, 16)
     for t in range(KT):
         q = g.sync if (is_owner or t % 2 == 0) else g.scalar
         q.dma_start(T.xb[:, 4 * NC * t:4 * NC * (t + 1)], T.x[:, 4 * NC * t:4 * NC * (t + 1)]).then_inc(S["xl%d" % t], 16)
-
     if is_owner:
         g.vector.wait_ge(S.wl, 16)
         g.vector.quantize_mx(T.wq[:], T.ws[:], T.wb[:]).then_inc(S.wqd, 1)
@@ -81,20 +113,17 @@ def rank_program(g, core, T, topo):
                              T.xb[:, 4 * NC * t:4 * NC * (t + 1)]).then_inc(S["xq%d" % t], 1)
 
     if core in plan:
-        if is_owner:
-            g.wait_ge(S.wqd, 1)
-        else:
-            g.wait_ge(S.warr, expect)
+        dsts, off, own, helpers = plan[core]
+        g.wait_ge(S.wqd, 1)
         left = 0
-        for dsts in plan[core]:
-            for d in dsts:
-                assert topo.may_write(core, d)
-            m = _mask(topo, core, dsts)
-            ids = [DstId(rid=topo.addr(d)[0], pnc=topo.addr(d)[1]) for d in dsts]
-            for ap in (T.wq[:].bitcast(dt.uint8), T.ws[:]):
-                g.remote_dma_fused([RemoteDMATransfer(dst_ids=ids, dma_engine_mask=m, remote_sem=S.warr,
-                                                      srcs=[ap], dsts=[ap for _ in dsts])], local_sem=S.sent)
-                left += _count(m)
+        g.remote_dma_fused([send(dsts, off, own[0], S.warr)], local_sem=S.sent)
+        left += _count(off)
+        if helpers:
+            g.remote_dma_fused([send([h], m, p, S.hand) for h, m, p in helpers], local_sem=S.sent)
+            left += sum(_count(m) for h, m, p in helpers)
+        for p in own[1:]:
+            g.remote_dma_fused([send(dsts, off, p, S.warr)], local_sem=S.sent)
+            left += _count(off)
         g.wait_ge(S.sent, left)
 
     if is_owner:

from concourse.bass import DstId, RemoteDMATransfer
from concourse.mybir import dt, ActivationFunctionType

KT = 3
WC = 128
NC = 512
BLOCKS = [(0, 256), (256, 256)]
PW = KT * WC // 4
SAME_DIE = [True, False]
OWN_WORDS = KT * WC - PW * (len(SAME_DIE) - 1)

SCRATCH = {
    "wb": ("sbuf", [128, KT * 4 * WC], "bfloat16"),
    "xb": ("sbuf", [128, KT * 4 * NC], "bfloat16"),
    "wq": ("sbuf", [128, KT * WC], "float8_e4m3fn_x4"),
    "ws": ("sbuf", [128, KT * WC], "uint8"),
    "xq": ("sbuf", [128, KT * NC], "float8_e4m3fn_x4"),
    "xs": ("sbuf", [128, KT * NC], "uint8"),
    "ps": ("psum", [128, 512 * len(BLOCKS)], "float32"),
    "yb": ("sbuf", [128, NC], "float32"),
}
SEMAPHORES = (["wl", "wqd", "warr", "hand", "sent"] + ["xl%d" % t for t in range(KT)] + ["xq%d" % t for t in range(KT)]
              + ["mm%d" % b for b in range(len(BLOCKS))] + ["cp%d" % b for b in range(len(BLOCKS))]
              + ["st%d" % b for b in range(len(BLOCKS))])


def _engines(mask):
    return [b for b in range(mask.bit_length()) if (mask >> b) & 1]


def _bits(engines):
    out = 0
    for b in engines:
        out |= 1 << b
    return out


def _count(mask):
    return bin(mask).count("1")


def _piece(T, p):
    kind, a, b = p
    return T.ws[:, a:b] if kind == "s" else T.wq[:, a:b].bitcast(dt.uint8)


def _plan(T, topo):
    cores, owner = list(T.cores), T.tables["OWNER"]
    plan = {}
    for o in sorted(set(owner)):
        src = cores[o]
        dsts = [cores[r] for r in range(len(cores)) if owner[r] == o and r != o]
        if not dsts:
            continue
        off = topo.mask(src, dsts[0])
        for d in dsts:
            off &= topo.mask(src, d)
        if len(dsts) < 3:
            plan[src] = (dsts, off, [("q", 0, KT * WC), ("s", 0, KT * WC)], [])
            continue
        pieces = [("s", 0, KT * WC)] + [("q", a, a + PW) for a in range(OWN_WORDS, KT * WC, PW)]
        helpers, used = [], []
        for same in SAME_DIE:
            h = [c for c in range(128) if topo.chip(c) == topo.chip(src) and c not in cores and c not in used
                 and (topo.die(c) == topo.die(src)) == same and all(topo.may_write(c, d) for d in dsts)][0]
            used.append(h)
        free = _engines(topo.mask(src, used[0]) & ~off)
        n = len(free) // len(used)
        for i, h in enumerate(used):
            helpers.append((h, _bits(free[n * i:n * (i + 1)]), pieces[i]))
        plan[src] = (dsts, off, [("q", 0, OWN_WORDS)], helpers)
    return plan


def rank_program(g, core, T, topo):
    plan = _plan(T, topo)
    rank = T.rank_of(core)
    S = T.sem

    def send(dsts, m, p, sem):
        for d in dsts:
            assert topo.may_write(core, d)
        ids = [DstId(rid=topo.addr(d)[0], pnc=topo.addr(d)[1]) for d in dsts]
        return RemoteDMATransfer(dst_ids=ids, dma_engine_mask=m, remote_sem=sem,
                                 srcs=[_piece(T, p)], dsts=[_piece(T, p) for _ in dsts])

    if rank is None:
        for src, (dsts, off, own, helpers) in plan.items():
            for h, m, p in helpers:
                if h == core:
                    g.wait_ge(S.hand, _count(m))
                    g.remote_dma_fused([send(dsts, off, p, S.warr)], local_sem=S.sent)
                    g.wait_ge(S.sent, _count(off))
        return

    is_owner = T.tables["OWNER"][rank] == rank
    expect = 0
    for src, (dsts, off, own, helpers) in plan.items():
        if core in dsts:
            expect = _count(off) * (len(own) + len(helpers))

    if is_owner:
        g.sync.dma_start(T.wb[:], T.w[:]).then_inc(S.wl, 16)
    for t in range(KT):
        q = g.sync if (is_owner or t % 2 == 0) else g.scalar
        q.dma_start(T.xb[:, 4 * NC * t:4 * NC * (t + 1)], T.x[:, 4 * NC * t:4 * NC * (t + 1)]).then_inc(S["xl%d" % t], 16)
    if is_owner:
        g.vector.wait_ge(S.wl, 16)
        g.vector.quantize_mx(T.wq[:], T.ws[:], T.wb[:]).then_inc(S.wqd, 1)
    for t in range(KT):
        g.vector.wait_ge(S["xl%d" % t], 16)
        g.vector.quantize_mx(T.xq[:, NC * t:NC * (t + 1)], T.xs[:, NC * t:NC * (t + 1)],
                             T.xb[:, 4 * NC * t:4 * NC * (t + 1)]).then_inc(S["xq%d" % t], 1)

    if core in plan:
        dsts, off, own, helpers = plan[core]
        g.wait_ge(S.wqd, 1)
        left = 0
        g.remote_dma_fused([send(dsts, off, own[0], S.warr)], local_sem=S.sent)
        left += _count(off)
        if helpers:
            g.remote_dma_fused([send([h], m, p, S.hand) for h, m, p in helpers], local_sem=S.sent)
            left += sum(_count(m) for h, m, p in helpers)
        for p in own[1:]:
            g.remote_dma_fused([send(dsts, off, p, S.warr)], local_sem=S.sent)
            left += _count(off)
        g.wait_ge(S.sent, left)

    if is_owner:
        g.tensor.wait_ge(S.wqd, 1)
    else:
        g.tensor.wait_ge(S.warr, expect)
    for b, (c0, n) in enumerate(BLOCKS):
        for t in range(KT):
            if b == 0:
                g.tensor.wait_ge(S["xq%d" % t], 1)
            mm = g.tensor.matmul_mx(T.ps[:, 512 * b:512 * b + n],
                                    T.wq[:, WC * t:WC * (t + 1)], T.ws[:, WC * t:WC * (t + 1)],
                                    T.xq[:, NC * t + c0:NC * t + c0 + n], T.xs[:, NC * t + c0:NC * t + c0 + n],
                                    t == 0, t == KT - 1)
        mm.then_inc(S["mm%d" % b], 1)
    for b, (c0, n) in enumerate(BLOCKS):
        mm, cp, st = S["mm%d" % b], S["cp%d" % b], S["st%d" % b]
        if b % 2 == 0:
            g.vector.wait_ge(mm, 1)
            g.vector.tensor_copy(T.yb[:, c0:c0 + n], T.ps[:, 512 * b:512 * b + n]).then_inc(cp, 1)
            q = g.sync
        else:
            g.scalar.wait_ge(mm, 1)
            g.scalar.activation(T.yb[:, c0:c0 + n], T.ps[:, 512 * b:512 * b + n],
                                ActivationFunctionType.Copy).then_inc(cp, 1)
            q = g.scalar
        q.wait_ge(cp, 1)
        q.dma_start(T.y[:, c0:c0 + n], T.yb[:, c0:c0 + n]).then_inc(st, 16)
    for b in range(len(BLOCKS)):
        (g.sync if b % 2 == 0 else g.scalar).wait_ge(S["st%d" % b], 16)
